import numpy as np, ml_dtypes
CORES = [9,25,41,57]
N = 4
BF = ml_dtypes.bfloat16
W, A, S, RO, H = 4096, 128, 4, 6, 2
def parts(rng):
    z = rng.integers(0, 256, (N, 8, 16, W)); w = rng.integers(0, 256, (N, 8, 16, 3)); w[..., 2] = rng.integers(0, 2048, (N, 8, 16))
    return z, w, rng.choice(np.array([750, 850, 950, 1200]), (N, 8, 1, 1))
def loose(rng):
    share = rng.choice(np.array([0.06, 0.15, 0.4, 0.9]), (N, 8, 1, A))
    return np.where(rng.random((N, 8, 16, A)) < share, rng.integers(0, W, (N, 8, 16, A)), -1)
def objects(rng, z, n):
    ix = np.argsort(rng.random((N, 8, W)), axis=-1)[..., :S * 2 * n]
    base = rng.integers(40, 216, (8, 16, 1, 1, n)); dev = rng.integers(-16, 17, (8, 16, 16, 2, n))
    order = np.argsort(rng.random((8, 16, n)), axis=1); rows = np.arange(16)[None, :, None]
    up = rows == order[:, :1]; down = rows == order[:, 1:2]
    v = base + np.where(up[:, None, :, None, :], 16, np.where(down[:, None, :, None, :], -16, dev))
    for q in range(N):
        np.put_along_axis(z[q], np.broadcast_to(ix[q][:, None, :], (8, 16, S * 2 * n)), v[:, :, S * q:S * q + S].reshape(8, 16, S * 2 * n), 2)
    return np.ascontiguousarray(ix.reshape(N, 8, S, 2, n).transpose(1, 0, 2, 3, 4)).reshape(8, 16, 2, n), up | down
def follow(rng, obj, am):
    out = []
    for r in range(N):
        c = rng.integers(0, obj.shape[-1], (8, 1, A))
        one = np.take_along_axis(obj[:, :, 0], c, 2); two = np.take_along_axis(obj[:, :, 1], c, 2); anchor = np.take_along_axis(am, c, 2)
        v = (rng.random((8, 16, A)) < rng.choice(np.array([0, 0, 0.1, 0.5]), (8, 1, A))) & ~anchor
        keep = anchor | (rng.random((8, 16, A)) < rng.random((8, 1, A)))
        out.append(np.where(keep, np.where(v, two, one), -1))
    return np.stack(out)
def pack(z, w, t, p, s):
    return {"tz": np.ascontiguousarray(z.reshape(N, 128, W)).astype(np.float32).astype(BF), "tp": np.ascontiguousarray(p.reshape(N, 128, A)).astype(np.int32),
            "sd": np.ascontiguousarray(s.reshape(N, 128, A)).astype(np.int32), "hw": np.ascontiguousarray(w.reshape(N, 128, 3)).astype(np.int32),
            "th": np.repeat(t.reshape(N, 8, 1), 16, axis=1).astype(np.int32)}
def setup_inputs(rng):
    z, w, t = parts(rng); obj, am = objects(rng, z, A // 4)
    p = np.where(rng.random((N, 8, 1, A)) < 0.5, follow(rng, obj, am), loose(rng))
    s = np.where(rng.random((N, 8, 1, A)) < 0.5, follow(rng, obj, am), loose(rng))
    return pack(z, w, t, p, s)
def setup_inputs_twins(rng):
    z, w, t = parts(rng); obj, am = objects(rng, z, 4); t[:] = 4096
    p = follow(rng, obj, am); p[:, 6:] = loose(rng)[:, 6:]; p[..., A // 2:] = p[..., :A // 2].copy()
    return pack(z, w, t, p, follow(rng, obj, am))
def setup_inputs_ties(rng):
    z, w, t = parts(rng)
    z = np.take_along_axis(rng.integers(0, 256, (N, 8, 16, 6)), rng.integers(0, 6, (N, 8, 1, W)), 3)
    t = rng.choice(np.array([1000, 4096]), (N, 8, 1, 1)); p = loose(rng); s = loose(rng)
    w[:, 0, :, :2] = 0; w[:, 1, :, 2] = 0; w[:, 4, :, 2] = rng.choice(np.array([5, 1031]), (N, 16)); t[:, :2] = 4096
    z[:, 2:4] = 100; t[::2, 2] = 0; t[1::2, 2] = 1; t[:, 3] = 432; p[:, 2:4, :, ::4] = -1
    return pack(z, w, t, p, s)
def setup_inputs_ends(rng):
    z = 255 * rng.integers(0, 2, (N, 8, 16, W)); ends = np.array([-1, 0, 1, W - 2, W - 1])
    p = rng.choice(ends, (N, 8, 16, A)); s = rng.choice(ends, (N, 8, 16, A)); t = rng.choice(np.array([0, 1, 2040, 4080, 4096]), (N, 8, 1, 1))
    w = rng.choice(np.array([0, 1, 254, 255]), (N, 8, 16, 3)); w[..., 2] = rng.choice(np.array([0, 1, 1025, 2046, 2047]), (N, 8, 16))
    p[:, 4] = rng.integers(0, W, (N, 16, A)); t[:, 4] = 4096
    z[:, 5] = 255; w[:, 5, :, :2] = 0; w[:, 5, 0, :2] = 255; w[:, 5, 1, :2] = 2; w[:, 5, :, 2] = 2047; t[:, 5] = 4096
    p[:, 6] = -1; t[:, 6] = 4096
    z[::2, 7] = 255; z[1::2, 7] = 0; p[:, 7] = rng.integers(0, W, (N, 16, A)); p[:, 7, (np.arange(16) // S) % 2 == 1] = -1
    t[1::4, 7] = 4081; t[3::4, 7] = 4080
    w[1::2, 7, :, 0] = 0; w[1::2, 7, :, 1] = 254 * rng.integers(0, 2, (N // 2, 16)); w[1::2, 7, 0, 1] = 255; w[1::2, 7, 0, 2] = rng.integers(1, 2048, N // 2)
    return pack(z, w, t, p, s)
def setup_inputs_sparse(rng):
    z, w, t = parts(rng); t = rng.choice(np.array([900, 4096]), (N, 8, 1, 1)); t[:, 0] = 4096
    p = np.where(rng.random((N, 8, 16, A)) < 0.06, rng.integers(0, W, (N, 8, 16, A)), -1); p[rng.integers(0, N)] = -1
    s = loose(rng); s[:, rng.permutation(8)[:4]] = -1
    return pack(z, w, t, p, s)
def setup_inputs_spread(rng):
    z = np.minimum((np.exp2(8.0 * rng.random((N, 8, 1, W))) * rng.random((N, 8, 16, W))).astype(np.int64), 255)
    w = np.minimum(np.exp2(8.0 * rng.random((N, 8, 16, 3))).astype(np.int64), 255); w[..., 2] = np.minimum(np.exp2(11.0 * rng.random((N, 8, 16))).astype(np.int64), 2047)
    t = np.minimum(np.exp2(7.0 + 5.0 * rng.random((N, 8, 1, 1))).astype(np.int64), 4096)
    ps = []
    for i in range(2):
        nm = np.minimum((W * rng.random((N, 8, 16, A)) ** 3).astype(np.int64), W - 1)
        ps.append(np.where(rng.random((N, 8, 16, A)) < rng.random((N, 8, 1, A)), nm, -1))
    return pack(z, w, t, ps[0], ps[1])
def check_inputs(d):
    bad = []; v = np.asarray(d["tz"]).astype(np.float32)
    if not (np.min(v) >= 0 and np.max(v) <= 255 and np.all(v == np.floor(v))): bad.append("tz: whole numbers from 0 to 255")
    for k, lo, hi in (("tp", -1, W - 1), ("sd", -1, W - 1), ("th", 0, 4096)):
        if np.min(d[k]) < lo or np.max(d[k]) > hi: bad.append("range of " + k)
    w = np.asarray(d["hw"])
    if np.min(w) < 0 or np.max(w[..., :2]) > 255 or np.max(w[..., 2]) > 2047: bad.append("range of hw")
    t = np.asarray(d["th"]).reshape(-1, 16)
    if np.any(t != t[:, :1]): bad.append("th: one number a group")
    return bad
def reference(tz, tp, sd, hw, th):
    z = tz.astype(np.float32).astype(np.int32).reshape(N, 8, 16, W); w = hw.astype(np.int32).reshape(N, 8, 16, 3); lim = th.astype(np.int32).reshape(N, 8, 16)[:, :, :1]
    p = tp.astype(np.int32).reshape(N, 8, 16, A); s = sd.astype(np.int32).reshape(N, 8, 16, A); lower = np.arange(A)[None, :] < np.arange(A)[:, None]
    for t in range(RO):
        for r in range(N):
            q = (r + 1 + t) % N; x = S * q + t // N
            hi = np.zeros((8, 16, A), np.int32); lo = np.full((8, 16, A), 255, np.int32)
            for j in range(16):
                n = p[r, :, j]; on = (n >= 0)[:, None, :]; v = np.take_along_axis(z[j // S], np.maximum(n, 0)[:, None, :], 2)
                hi = np.where(on, np.maximum(hi, v), hi); lo = np.where(on, np.minimum(lo, v), lo)
            e = (hi + lo) >> 1; c = e
            best = np.full((8, A), 4097); name = np.zeros((8, A), np.int64)
            for k in range(H):
                u1 = np.add.reduce(w[q, :, :, 0:1] * c, axis=1) & (W - 1); u2 = np.add.reduce(w[q, :, :, 1:2] * c, axis=1) & (W - 1)
                h = (((u1 * u2) >> 5)[:, None, :] + w[q, :, :, 2:3] * u2[:, None, :]) & (W - 1)
                v = np.take_along_axis(z[q], h.reshape(8, 1, 16 * A), 2).reshape(8, 16, 16, A)
                d = np.add.reduce(np.abs(v - e[:, :, None, :]), axis=1)
                m = np.argmin(d, axis=1); dm = np.min(d, axis=1); n = np.take_along_axis(h, m[:, None, :], 1)[:, 0]
                less = dm < best; name = np.where(less, n, name); best = np.where(less, dm, best)
                c = (e + np.take_along_axis(z[q], n[:, None, :], 2)) >> 1
            n = np.where(best < lim[q], name, -1); p[r, :, x] = n
            low = (n[:, :, None] == n[:, None, :]) & (n >= 0)[:, :, None] & lower
            g, b = np.nonzero(np.count_nonzero(low, axis=2) == 1); a = np.argmax(low[g, b], axis=1)
            pa = p[r][g, :, a]; pb = p[r][g, :, b]; differ = (pa >= 0) & (pb >= 0) & (pa != pb); clash = np.any(differ, axis=1)[:, None]
            p[r][g, :, a] = np.where(clash, np.where(differ, -1, pa), np.where(pa >= 0, pa, pb))
            p[r][g, :, b] = np.where(clash, np.where(differ, -1, pb), s[r][g, :, b])
    return {"yp": p.reshape(N, 128, A).astype(np.float32)}

import numpy as np
from concourse.bass import DstId, RemoteDMATransfer
from concourse.mybir import AluOpType as O, ActivationFunctionType as F

N, W, A, S, RO = 4, 4096, 128, 4, 6
BLK = W + 16
M1, M4, M12 = 1.5 * 2.0 ** 24, 1.5 * 2.0 ** 27, 1.5 * 2.0 ** 35
SPLIT_E = 72
SPLIT_V = 64
OWN = [(0, 1088), (1088, 2176)]
HELP = [(2176, 3136), (3136, 4096)]

SCRATCH = {}
for _n, _c, _d in (
        ("zall", N * BLK, "bfloat16"), ("zh", HELP[-1][1] - HELP[0][0], "bfloat16"), ("hwi", 16, "int32"), ("hwf", 16, "float32"),
        ("tpi", 256, "int32"), ("tpf", 256, "float32"), ("P", 256, "float32"), ("Pw", 256, "float32"), ("Pm", 128, "float32"),
        ("Q", 256, "float32"), ("offs", 128, "uint16"), ("hl", 128, "uint16"), ("l0", 8, "uint16"), ("L", 8, "uint16"),
        ("Ve", 2048, "bfloat16"), ("Va", 2048, "bfloat16"), ("Hi", 2048, "bfloat16"), ("Lo", 2048, "bfloat16"),
        ("V", 2048, "bfloat16"), ("Mx", 2048, "bfloat16"), ("E2", 128, "bfloat16"), ("C2", 128, "bfloat16"), ("Epl", 128, "float32"),
        ("cs", 128, "float32"), ("uq", 256, "float32"), ("u1", 128, "float32"), ("pr", 128, "int32"), ("sh", 128, "int32"),
        ("sm", 128, "int32"), ("hn", 128, "int32"), ("G", 256, "float16"), ("km", 128, "float32"), ("q8", 8, "float32"),
        ("Zb", 128, "bfloat16"), ("Ze", 128, "bfloat16"), ("Zm", 128, "bfloat16"), ("kf0", 8, "float32"), ("Zf", 128, "float32"),
        ("kfr", 128, "float32"), ("OH", 256, "bfloat16"), ("pd", 256, "float16"), ("SU", 128, "bfloat16"), ("Ux", 128, "float16"),
        ("rs", 128, "float16"), ("nc", 8, "float32"), ("X", 1024, "bfloat16"), ("iM", 128, "bfloat16"), ("iU", 128, "bfloat16"),
        ("vl", 128, "bfloat16"), ("mn", 128, "float32"), ("aa", 128, "float32"), ("dif", 128, "bfloat16"), ("sB", 128, "float32"),
        ("B0", 128, "float32"), ("B1", 128, "float32"), ("y0", 128, "float32"), ("y1", 128, "float32"), ("y2", 128, "float32"),
        ("on", 128, "bfloat16"), ("BD", 128, "bfloat16"), ("Ib", 128, "bfloat16"), ("If", 128, "float32"), ("onf", 128, "float32"),
        ("HI", 128, "bfloat16"), ("NH", 128, "bfloat16"), ("CU", 256, "bfloat16"), ("BDE", 128, "bfloat16"), ("IV", 8, "bfloat16"),
        ("IM", 8, "bfloat16"), ("I1", 8, "bfloat16"), ("Ih", 8, "float16"), ("I16", 8, "float32"), ("thx", 32, "float32"),
        ("TH", 32, "float32"), ("W1", 512, "bfloat16"), ("W2", 512, "bfloat16"), ("KC", 256, "bfloat16"), ("d0h", 2048, "bfloat16"),
        ("d0l", 2048, "bfloat16"), ("d0k", 128, "float32"), ("s1b", 128, "bfloat16"), ("s1f", 128, "float32"), ("CT1", 8, "float32"),
        ("CT2", 8, "bfloat16"), ("CC", 384, "bfloat16"), ("Wt", 48, "bfloat16"), ("MB", 512, "bfloat16"), ("GO", 1024, "float16"),
        ("Sx", 768, "float16"), ("zb", 768, "bfloat16"), ("N4", 128, "bfloat16"), ("C32", 128, "bfloat16"), ("CSX", 256, "bfloat16"),
        ("IP", 128, "bfloat16"), ("IN", 128, "bfloat16"), ("CAB", 256, "bfloat16"), ("cA", 128, "bfloat16"), ("cB", 128, "bfloat16"),
        ("Uf", 128, "float32"), ("jc", 1, "float32"), ("bc", 1, "float32"), ("rx", 8, "float32"), ("cx", 8, "float32"),
        ("ji", 128, "int32"), ("jj", 128, "int32"), ("jk", 128, "int32"), ("mf", 128, "float32"), ("t8", 8, "float32")):
    SCRATCH[_n] = ("sbuf", [128, _c], _d)
BANKS = ("bV", "bA", "bB", "bE", "bK0", "bK1", "bR0", "bR1")
for _n in BANKS:
    SCRATCH[_n] = ("psum", [128, 512], "float32")
SEMAPHORES = (["cV", "cS", "cT", "cG", "ldp", "ldh", "st", "lsem"] + ["ld%d" % i for i in range(4)] + ["tz%d" % i for i in range(N)]
              + ["hw%d" % i for i in range(N)] + ["hx%d" % i for i in range(len(HELP))])


def Tracker(g, T):
    eng = {"V": g.vector, "S": g.scalar, "T": g.tensor, "G": g, "Y": g.sync}
    cnt = {e: 0 for e in eng}; know = {e: {} for e in eng}; snap = {}; acc = {}

    def need(e, needs):
        while True:
            todo = {s: n for s, n in needs.items() if know[e].get(s, 0) < n}
            if not todo:
                return
            s = max(todo, key=lambda k: sum(1 for j in todo if j != k and snap.get((k, todo[k]), {}).get(j, 0) >= todo[j]))
            n = todo[s]
            eng[e].wait_ge(T.sem[s], n)
            for k, v in snap.get((s, n), {}).items():
                know[e][k] = max(know[e].get(k, 0), v)
            know[e][s] = max(know[e].get(s, 0), n)

    def conflicts(e, refs, write, needs):
        for nm, lo, hi, st in refs:
            bank = nm in BANKS
            for w, ee, s, n, l2, h2, st2 in acc.get(nm, ()):
                over = lo < h2 and l2 < hi and not (st == st2 > 1 and (lo - l2) % st)
                if ee == e:
                    hit = over and w and not (e == "T" and bank)
                else:
                    hit = bank or (over and (w or write))
                if hit:
                    needs[s] = max(needs.get(s, 0), n)

    def note(e, s, n, refs, write):
        for nm, lo, hi, st in refs:
            keep = []
            for a in acc.get(nm, ()):
                cover = lo <= a[4] and a[5] <= hi and (st == 1 or (st == a[6] and (lo - a[4]) % st == 0))
                if not (cover and (write or (not a[0] and a[1] == e))):
                    keep.append(a)
            acc[nm] = keep + [(write, e, s, n, lo, hi, st)]

    def ref(r):
        return (r[0], r[1], r[2], r[3] if len(r) > 3 else 1)

    def ap(r):
        return T[r[0]][:, r[1]:r[2]:r[3]] if len(r) > 3 else T[r[0]][:, r[1]:r[2]]

    def op(e, outs, ins, call):
        needs = {}
        ro, ri = [ref(r) for r in outs], [ref(r) for r in ins]
        conflicts(e, ri, False, needs)
        conflicts(e, ro, True, needs)
        need(e, needs)
        cnt[e] += 1
        s = "c" + e
        snap[(s, cnt[e])] = dict(know[e])
        call().then_inc(T.sem[s], 1)
        note(e, s, cnt[e], ri, False)
        note(e, s, cnt[e], ro, True)

    def landed(sem, n, refs):
        note("dma", sem, n, [ref(r) for r in refs], True)

    def before(e, ins):
        needs = {}
        conflicts(e, [ref(r) for r in ins], False, needs)
        need(e, needs)
    return {"op": op, "ap": ap, "landed": landed, "before": before, "cnt": cnt, "need": need}


def rank_program(g, core, T, topo):
    rank = T.rank_of(core)
    helpers = []
    for c in T.cores:
        helpers.append([k for k in topo.cores_of(c) if topo.die(k) != topo.die(c) and k not in T.cores
                        and all(topo.may_write(k, d) for d in T.cores if d != c)][0])
    if rank is None:
        if core in helpers:
            helper_program(g, core, T, topo, helpers.index(core))
        return
    others = [c for c in T.cores if c != core]
    K = Tracker(g, T)
    op, ap = K["op"], K["ap"]

    def ind(win, off):
        return ap(win).indirect(ap(off))

    def tt(out, a, b, o, win=None):
        op("V", [out], [a, b] + ([win] if win else []), lambda: g.vector.tensor_tensor(ap(out), ind(win, a) if win else ap(a), ap(b), o))

    def ts(out, a, s1, o1, s2=None, o2=None):
        ins = [a] + [s for s in (s1, s2) if isinstance(s, tuple)]
        f = lambda s: ap(s) if isinstance(s, tuple) else s
        if o2 is None:
            op("V", [out], ins, lambda: g.vector.tensor_scalar(ap(out), ap(a), f(s1), None, o1))
        else:
            op("V", [out], ins, lambda: g.vector.tensor_scalar(ap(out), ap(a), f(s1), f(s2), o1, o2))

    def cp(out, a):
        op("V", [out], [a], lambda: g.vector.tensor_copy(ap(out), ap(a)))

    def gat(out, win, off):
        op("V", [out], [win, off], lambda: g.vector.tensor_copy(ap(out), ind(win, off)))

    def sgat(out, win, off):
        op("S", [out], [win, off], lambda: g.scalar.activation(ap(out), ind(win, off), F.Copy))

    def scat(win, off, a):
        op("V", [win], [off, a], lambda: g.vector.tensor_copy(ind(win, off), ap(a)))

    def scan(out, d0, d1, o0, o1):
        op("V", [out], [d0, d1], lambda: g.vector.tensor_tensor_scan(ap(out), ap(d0), ap(d1), 0.0, o0, o1))

    def fill(out, c, p0=0, p1=128):
        op("V", [out], [], lambda: g.vector.memset(T[out[0]][p0:p1, out[1]:out[2]] if len(out) < 4 else ap(out), c))

    def mm(out, l, r, start, stop):
        op("T", [out], [l, r], lambda: g.tensor.matmul(ap(out), ap(l), ap(r), start, stop))

    def act(out, a, f, **k):
        op("S", [out], [a], lambda: g.scalar.activation(ap(out), ap(a), f, **k))

    def sel(out, a, pattern, o, base, cm):
        op("G", [out], [a], lambda: g.affine_select(ap(out), ap(a), pattern, o, 0.0, base, cm))

    def iota(out, pattern, base, cm, **k):
        op("G", [out], [], lambda: g.iota(ap(out), pattern, base, cm, **k))

    def b(n, lo=0, hi=128, *st):
        return (n, lo, hi) + st
    BM, PS, X1, X2 = [("bV", 128 * i, 128 * i + 128) for i in range(4)]
    fl = {"allow_small_or_imprecise_dtypes": True}

    base = rank * BLK
    chunks = [HELP[0], OWN[0], HELP[1], OWN[1]]
    for i, (c0, c1) in enumerate(chunks):
        q = g.sync if i % 2 == 0 else g.scalar
        q.dma_start(T.zall[:, base + c0:base + c1], T.tz[:, c0:c1]).then_inc(T.sem["ld%d" % i], 16)
        K["landed"]("ld%d" % i, 16, [("zall", base + c0, base + c1)])
    g.scalar.dma_start(T.hwi[:, 4 * rank:4 * rank + 3], T.hw[:, :]).then_inc(T.sem.ldh, 16)
    g.scalar.dma_start(T.hwi[:, 4 * rank + 3:4 * rank + 4], T.th[:, :]).then_inc(T.sem.ldh, 16)
    g.sync.dma_start(T.tpi[:, 0:128], T.tp[:, :]).then_inc(T.sem.ldp, 16)
    g.sync.dma_start(T.tpi[:, 128:256], T.sd[:, :]).then_inc(T.sem.ldp, 16)
    K["landed"]("ldh", 32, [("hwi", 4 * rank, 4 * rank + 4)])
    K["landed"]("ldp", 32, [("tpi", 0, 256)])

    fill(b("on"), 1.0)
    fill(b("onf"), 1.0)
    sel(b("OH"), b("on"), [[-16, 8], [0, 16]], O.is_ge, 0, 1)
    sel(b("BD"), b("OH"), [[16, 8], [0, 16]], O.is_ge, 15, -1)
    sel(b("If"), b("onf"), [[-1, 128]], O.is_equal, 0, 1)

    h = helpers[rank]
    spare = [e for e in topo.engines(core, h) if e not in topo.engines(core, others[0])]
    eo = len(topo.engines(core, others[0]))
    local = 0
    to = [DstId(rid=topo.addr(c)[0], pnc=topo.addr(c)[1]) for c in others]

    def to_others(buf, lo, hi, sem):
        t = RemoteDMATransfer(dst_ids=to, dma_engine_mask=topo.mask(core, others[0]), remote_sem=T.sem[sem],
                              srcs=[T[buf][:, lo:hi]], dsts=[T[buf][:, lo:hi] for _ in others])
        g.remote_dma_fused([t], local_sem=T.sem.lsem)
        return eo
    for i, (c0, c1) in enumerate(chunks):
        K["before"]("G", [("zall", base + c0, base + c1)])
        if i % 2 == 0:
            t = RemoteDMATransfer(dst_ids=[DstId(rid=topo.addr(h)[0], pnc=topo.addr(h)[1])], dma_engine_mask=sum(1 << e for e in spare),
                                  remote_sem=T.sem["hx%d" % (i // 2)], srcs=[T.zall[:, base + c0:base + c1]],
                                  dsts=[T.zh[:, c0 - HELP[0][0]:c1 - HELP[0][0]]])
            g.remote_dma_fused([t], local_sem=T.sem.lsem)
            local += len(spare)
        else:
            local += to_others("zall", base + c0, base + c1, "tz%d" % rank)
        if i == 1:
            K["before"]("G", [("hwi", 4 * rank, 4 * rank + 4)])
            local += to_others("hwi", 4 * rank, 4 * rank + 4, "hw%d" % rank)
    for q in range(N):
        if q != rank:
            K["landed"]("tz%d" % q, eo * (len(OWN) + len(HELP)), [("zall", q * BLK, q * BLK + W)])
            K["landed"]("hw%d" % q, eo, [("hwi", 4 * q, 4 * q + 4)])

    iota(b("ji"), [[0, 8], [-1, 16]], 128, 1)
    iota(b("KC"), [[0, 8], [1, 16]], 0, 0, **fl)
    iota(b("CT1", 0, 8), [[16, 8]], 0, 1, **fl)
    iota(b("Uf"), [[16, 128]], 2050, 0, **fl)
    iota(b("y0"), [[0, 128]], 0, 1, **fl)
    fill(b("y1"), 8192.0)
    sel(b("y2"), b("y1"), [[-1, 128]], O.is_ge, 0, 1)
    for q in range(N):
        fill(b("zall", q * BLK + W, (q + 1) * BLK), -256.0)
    for nm, w, lo, hi in (("d0h", 2048, 255.0, 0.0), ("d0l", 2048, 0.0, 255.0), ("d0k", 128, -1.0e9, 1.0e9), ("s1b", 128, 1.0, 0.0), ("s1f", 128, 1.0, 0.0)):
        fill(b(nm, 0, w), lo)
        fill(b(nm, 0, w, 16), hi)
    for nm, w in (("Zb", 128), ("Zf", 128), ("SU", 128), ("Q", 256), ("zb", 768)):
        fill(b(nm, 0, w), 0.0)
    fill(b("NH"), -0.5)
    fill(b("CU", 0, 256), -16.0)
    fill(b("CU", 0, 256), -15.5, 0, 1)
    fill(b("C32"), 32.0)
    fill(b("CSX"), -16384.0); fill(b("CSX", 128, 256), 16384.0)
    fill(b("CAB"), 8192.0); fill(b("CAB", 128, 256), -8192.0)
    cp(b("Ib"), b("If"))
    for nm, c in (("HI", 0.5), ("IP", 32768.0), ("IN", -32768.0), ("N4", -4096.0)):
        ts(b(nm), b("Ib"), c, O.mult)
    bd16 = b("BD", 0, 128, 16)
    ts(b("BDE"), b("BD"), -16.0, O.mult)
    ts(b("cB"), b("BD"), 16384.0, O.mult)
    for nm, c in (("IV", -32.0), ("IM", 64.0), ("I1", 1.0), ("Ih", 1.0), ("I16", 0.0625)):
        ts(b(nm, 0, 8), bd16, c, O.mult)
    ts(b("mn"), b("If"), 262144.0, O.mult)
    ts(b("mf"), b("BD"), -16384.0, O.mult)
    tt(b("cA"), b("mn"), b("mf"), O.add)
    for i in range(8):
        ts(b("GO", 128 * i, 128 * i + 128), b("on"), b("BD", 16 * i, 16 * i + 1), O.mult)
    for i in range(4):
        cp(b("MB", 128 * i, 128 * i + 128), b("y2"))
    ts(b("jj"), b("ji"), 15, O.bitwise_and)
    ts(BM, b("jj"), 0, O.is_equal)
    ts(b("mf"), b("jj"), 0, O.is_equal)
    cp(b("jc", 0, 1), b("jj", 0, 1))
    ts(b("jk", 0, 1), b("jj", 0, 1), 2, O.arith_shift_right)
    ts(b("bc", 0, 1), b("jk", 0, 1), float(BLK), O.mult, 2048.0, O.add)
    xs = [S * ((rank + 1 + t) % N) + t // N for t in range(RO)]
    cp(b("Sx", 0, 768), b("zb", 0, 768))
    for t, x in enumerate(xs):
        ts(b("rx", t, t + 1), b("jc", 0, 1), float(x), O.is_equal)
        ts(b("cx", t, t + 1), b("rx", t, t + 1), 8192.0, O.mult, -4096.0, O.add)
        cp(b("Sx", 128 * t + x, 128 * t + 128, 16), b("BD", x, 128, 16))
    ts(b("KC", 128, 256), b("KC"), 8.5, O.add)
    ts(b("KC"), b("KC"), -7.5, O.add)
    tt(b("t8", 0, 1), b("y0", 0, 1), b("jc", 0, 1), O.subtract)
    ts(b("q8", 0, 8), b("CT1", 0, 8), b("t8", 0, 1), O.subtract)
    ts(b("CT2", 0, 8), b("q8", 0, 8), 128.0, O.add)
    ts(b("CT1", 0, 8), b("q8", 0, 8), 16.0, O.mult, 7.5, O.add)
    ts(b("CC", 0, 384, 3), b("mf"), -4.0, O.mult, 4.0, O.add)
    ts(b("CC", 1, 384, 3), b("y0"), -1.0, O.mult)
    ts(b("CC", 2, 384, 3), b("y0"), 0.0, O.mult)
    fill(b("Wt", 0, 48), 1.0)
    ts(b("Wt", 1, 48, 3), b("y0", 0, 16), -128.0, O.add)
    ts(b("tpf", 0, 256), b("tpi", 0, 256), 0, O.is_lt, 8192.0, O.mult)
    ts(b("Pw", 0, 256), b("tpi", 0, 256), -2048, O.add)
    tt(b("P", 0, 256), b("Pw", 0, 256), b("tpf", 0, 256), O.add)
    SD = b("P", 128, 256)
    for q in [rank] + [(rank + i) % N for i in range(1, N)]:
        cp(b("hwf", 4 * q, 4 * q + 4), b("hwi", 4 * q, 4 * q + 4))
        ts(b("W1", 128 * q, 128 * q + 128), b("BD"), b("hwf", 4 * q, 4 * q + 1), O.mult, 0.5, O.mult)
        ts(b("W2", 128 * q, 128 * q + 128), b("BD"), b("hwf", 4 * q + 1, 4 * q + 2), O.mult, 0.5, O.mult)
        ts(b("thx", 8 * q, 8 * q + 8), b("I16", 0, 8), b("hwf", 4 * q + 3, 4 * q + 4), O.mult)
    mm(b("bA", 0, 32), b("onf"), b("thx", 0, 32), True, True)
    ts(b("TH", 0, 32), b("bA", 0, 32), 32.0, O.mult, -7.75, O.add)

    def hash_mm(C, q):
        mm(b("bA", 0, 256), b("on"), b("CU", 0, 256), True, False)
        w1, w2 = b("W1", 128 * q, 128 * q + 128), b("W2", 128 * q, 128 * q + 128)
        mm(b("bA", 0, 128), w1, b(C), False, False)
        mm(b("bA", 128, 256), w2, b(C), False, True)
        mm(b("bB", 0, 128), w1, b(C), True, True)
        mm(b("bB", 128, 256), w2, b(C), True, True)

    def hash_v(q):
        ts(b("uq", 0, 256), b("bA", 0, 256), M12, O.add, -M12, O.add)
        tt(b("u1"), b("bB", 0, 128), b("uq", 0, 128), O.subtract)
        tt(X1, b("bB", 128, 256), b("uq", 128, 256), O.subtract)
        tt(b("pr"), b("u1"), X1, O.mult)
        ts(X2, X1, b("hwf", 4 * q + 2, 4 * q + 3), O.mult)
        ts(b("sh"), b("pr"), 5, O.arith_shift_right)
        tt(b("sm"), b("sh"), X2, O.add)
        ts(b("hn"), b("sm"), 4095, O.bitwise_and)
        cp(b("hl"), b("hn"))

    def search(q, p):
        win = b("zall", q * BLK, q * BLK + W)
        c = 16 * SPLIT_V
        sgat(b("V", c, 2048), win, b("hl", SPLIT_V, 128))
        gat(b("V", 0, c), win, b("hl", 0, SPLIT_V))
        ts(b("G", 128 * p, 128 * p + 128), b("hn"), -2048.0, O.add)
        bk = "bK%d" % p

        def vm(m):
            mm(b(bk, m, 128, 16), b("V", m, 2048, 16), b("IV", 0, 8), False, False)
        vm(0)
        vm(1)
        for m in range(16):
            tt(b("Mx", m, 2048, 16), b("V", m, 2048, 16), b("bE"), O.max)
            mm(b(bk, m, 128, 16), b("Mx", m, 2048, 16), b("IM", 0, 8), False, m == 15)
            if m < 14:
                vm(m + 2)

    def key_mm(p):
        mm(b("bK%d" % p), b("Ib"), b("KC", 128 * p, 128 * p + 128), True, False)
        mm(b("bK%d" % p), b("E2"), b("BDE"), False, False)

    for t in range(RO):
        q = (rank + 1 + t) % N
        x = xs[t]
        km8, th8, z16 = b("km", 15, 128, 16), b("TH", 8 * q, 8 * q + 8), b("Zf", 0, 128, 16)
        ts(b("offs"), b("P"), 2048.0, O.min, b("bc", 0, 1), O.add)
        c, h2 = 16 * SPLIT_E, 8 * SPLIT_E
        sgat(b("Ve", c, 2048), b("zall", 0, N * BLK), b("offs", SPLIT_E, 128))
        gat(b("Ve", 0, c), b("zall", 0, N * BLK), b("offs", 0, SPLIT_E))
        mm(b("bE", 128, 256), b("Ib"), b("NH"), True, False)
        pieces = [(c, 2048), (0, h2), (h2, c)]
        for lo, hi in pieces:
            act(b("Va", lo, hi), b("Ve", lo, hi), F.Abs)
        for lo, hi in ((0, c), (c, 2048)):
            scan(b("Hi", lo, hi), b("d0h", lo, hi), b("Ve", lo, hi), O.min, O.max)
        for lo, hi in pieces:
            scan(b("Lo", lo, hi), b("d0l", lo, hi), b("Va", lo, hi), O.max, O.min)
        mm(b("bE", 128, 256), b("Ib"), b("Hi", 15, 2048, 16), False, False)
        mm(b("bE", 128, 256), b("Ib"), b("Lo", 15, 2048, 16), False, True)
        ts(b("E2"), b("bE", 128, 256), M1, O.add, -M1, O.add)
        act(b("Epl"), b("E2"), F.Identity, scale=0.5, bias=-0.5)
        hash_mm("E2", q)
        mm(b("bE"), b("HI"), b("E2"), True, True)
        key_mm(0)
        ts(b("Pm"), b("P"), b("cx", t, t + 1), O.max)
        hash_v(q)
        search(q, 0)
        scan(b("km"), b("d0k"), b("bK0"), O.max, O.min)
        ts(b("q8", 0, 8), km8, M4, O.add, -M4, O.add)
        tt(b("Zb", 0, 128, 16), km8, b("q8", 0, 8), O.subtract)
        scan(b("Ze"), b("s1b"), b("Zb"), O.mult, O.add)
        tt(b("Zm"), b("Ze"), BM, O.mult)
        mm(b("bA", 256, 264), b("If"), b("CT1", 0, 8), True, False)
        mm(b("bA", 256, 264), b("Zm"), b("I1", 0, 8), False, True)
        key_mm(1)
        mm(b("bR0", 0, 512), b("Ib"), b("MB", 0, 512), True, False)
        mm(b("bR1", 0, 512), b("Ib"), b("MB", 0, 512), True, False)
        tt(b("kf0", 0, 8), km8, th8, O.min)
        cp(b("l0", 0, 8), b("bA", 256, 264))
        tt(b("cs"), b("l0", 0, 8), b("Epl"), O.add, win=b("V", 0, 2048))
        ts(b("C2"), b("cs"), M1, O.add, -M1, O.add)
        hash_mm("C2", q)
        fill(b("SU"), 0.0)
        ts(b("Ux"), b("Uf"), b("rx", t, t + 1), O.mult)
        hash_v(q)
        search(q, 1)
        scan(b("km"), b("d0k"), b("bK1"), O.max, O.min)
        tt(z16, km8, b("kf0", 0, 8), O.min)
        scan(b("kfr"), b("s1f"), b("Zf"), O.mult, O.add)
        tt(b("OH"), b("kfr"), b("bK0"), O.is_equal)
        tt(b("OH", 128, 256), b("kfr"), b("bK1"), O.is_equal)
        tt(b("SU", x, 128, 16), z16, th8, O.is_lt)
        mm(b("bA", 0, 128), b("OH"), b("Ib"), True, True)
        mm(b("bE"), b("OH", 128, 256), b("Ib"), True, True)
        tt(b("pd"), b("bA"), b("G"), O.mult)
        tt(b("pd", 128, 256), b("bE"), b("G", 128, 256), O.mult)
        sx = b("Sx", 128 * t, 128 * t + 128)
        mm(b("bB"), b("on"), b("C32"), True, False)
        mm(b("bB"), b("SU"), b("N4"), False, False)
        mm(b("bB"), sx, b("pd"), False, False)
        mm(b("bB"), sx, b("pd", 128, 256), False, True)
        mm(b("bK0", 0, 384), b("Ib"), b("CC", 0, 384), True, False)
        tt(b("rs"), b("bB"), b("Ux"), O.min)
        mm(b("bA", 0, 8), b("rs"), b("Ih", 0, 8), True, True)
        for i in range(8):
            mm(b("bR%d" % (i // 4), 128 * (i % 4), 128 * (i % 4) + 128), b("GO", 128 * i, 128 * i + 128), b("rs"), False, i % 4 == 3)
        tt(b("Pw"), b("Pm"), b("bB"), O.min)
        tt(b("Pw", 128, 256), b("Pm"), b("bB"), O.min)
        tt(PS, b("Pm"), b("bB"), O.min)
        cp(b("nc", 0, 8), b("bA", 0, 8))
        for i in range(8):
            xg = b("X", 128 * i, 128 * i + 128)
            ts(xg, b("bR%d" % (i // 4), 128 * (i % 4), 128 * (i % 4) + 128), b("nc", i, i + 1), O.is_equal)
            mm(b("bK0", 48 * i, 48 * i + 48), xg, b("Wt", 0, 48), False, i == 7)
        mm(b("bA", 256, 264), b("Ib"), b("CT2", 0, 8), True, False)
        ts(b("iM"), b("bK0", 0, 384, 3), 1.0, O.is_equal)
        tt(b("vl"), b("iM"), b("bK0", 1, 384, 3), O.mult)
        mm(b("bA", 256, 264), b("vl"), b("I1", 0, 8), False, True)
        ts(b("iU"), b("bK0", 2, 384, 3), 1.0, O.is_equal)
        mm(b("bK1", 0, 256), b("Ib"), b("CSX", 0, 256), True, False)
        mm(b("bK1", 0, 128), b("iU"), b("IP"), False, False)
        mm(b("bK1", 128, 256), b("iU"), b("IN"), False, True)
        mm(b("bB", 0, 256), b("Ib"), b("CAB", 0, 256), True, False)
        cp(b("L", 0, 8), b("bA", 256, 264))
        gat(b("Q"), b("Pw", 0, 256), b("L", 0, 8))
        scat(b("Q", 0, 256), b("L", 0, 8), b("Pw"))
        tt(b("sB"), SD, b("bK1", 128, 256), O.max)
        tt(X1, b("Q"), PS, O.max)
        tt(b("mn"), b("Q"), PS, O.min)
        ts(X2, X1, 2048.0, O.is_lt)
        tt(b("aa"), X1, b("mn"), O.subtract)
        tt(b("dif"), b("aa"), X2, O.min)
        mm(b("bB", 0, 128), b("cA"), b("dif"), False, False)
        mm(b("bB", 128, 256), b("cB"), b("dif"), False, True)
        tt(X1, b("mn"), b("bK1", 0, 128), O.max)
        tt(b("B0"), b("sB"), X1, O.min)
        tt(X2, b("Pw"), b("bB", 0, 128), O.max)
        tt(b("B1"), b("B0"), b("bB", 128, 256), O.max)
        tt(b("P"), b("B1"), X2, O.min)
    ts(b("y0"), b("P"), 4096.0, O.min, 2049.0, O.add)
    ts(b("y1"), b("P"), 2048.0, O.is_lt)
    tt(b("y2"), b("y0"), b("y1"), O.mult)
    ts(b("B0"), b("y2"), -1.0, O.add)
    K["before"]("Y", [b("B0")])
    g.sync.dma_start(T.yp[:, :], T.B0[:, :]).then_inc(T.sem.st, 16)
    K["need"]("Y", {"c" + e: K["cnt"][e] for e in "VSTG"})
    g.sync.wait_ge(T.sem.st, 16)
    g.wait_ge(T.sem.lsem, local)


def helper_program(g, core, T, topo, r):
    dests = [c for i, c in enumerate(T.cores) if i != r]
    n_in = len([e for e in topo.engines(T.cores[r], core) if e not in topo.engines(T.cores[r], dests[0])])
    ids = [DstId(rid=topo.addr(c)[0], pnc=topo.addr(c)[1]) for c in dests]
    o = HELP[0][0]
    for i, (c0, c1) in enumerate(HELP):
        g.wait_ge(T.sem["hx%d" % i], n_in)
        t = RemoteDMATransfer(dst_ids=ids, dma_engine_mask=topo.mask(core, dests[0]), remote_sem=T.sem["tz%d" % r],
                              srcs=[T.zh[:, c0 - o:c1 - o]], dsts=[T.zall[:, r * BLK + c0:r * BLK + c1] for _ in dests])
        g.remote_dma_fused([t], local_sem=T.sem.lsem)
    g.wait_ge(T.sem.lsem, len(HELP) * len(topo.engines(core, dests[0])))
